import numpy as np
import ml_dtypes


def mxq(x, axis, fmt="e4m3"):
    dtype, down = {"e4m3": (ml_dtypes.float8_e4m3fn, 7), "e5m2": (ml_dtypes.float8_e5m2, 14)}[fmt]
    v = np.moveaxis(np.asarray(x, np.float32).astype(ml_dtypes.bfloat16).astype(np.float64), axis, -1)
    blocks = v.reshape(v.shape[:-1] + (-1, 32))
    amax = np.abs(blocks).max(-1, keepdims=True)
    byte = np.maximum(np.where(amax > 0, np.frexp(amax)[1] - 1 + 127, 0) - down, 1)
    scale = np.exp2(byte - 127.0)
    codes = (blocks / scale).astype(np.float32).astype(dtype).astype(np.float64)
    return np.moveaxis((codes * scale).reshape(v.shape), -1, axis)


WIDE = False


def mx_kscale(k):
    if not WIDE:
        return np.ones(k)
    levels = np.array([30, -30])
    if k % 512:
        return np.exp2(np.random.permutation(np.resize(levels, k // 32))).repeat(32)
    a = np.empty((k // 512, 16))
    for p in range(k // 512):
        a[p, :8] = np.random.permutation(np.resize(levels, 8))
        for g in range(8):
            far = levels[np.abs(levels - a[p, g]) >= 10]
            a[p, g + 8] = far[np.random.randint(len(far))]
    return np.exp2(a.ravel()).repeat(32)


def f64(x):
    return np.asarray(x).astype(np.float64)


def striped(idx):
    return np.tile(np.asarray(idx).reshape(-1, 16).T, (8, 1)).astype(np.uint16)


def unstriped(offs):
    return offs[:16].T.reshape(-1).astype(np.int64)


E2M1 = np.array([0.0, 0.5, 1.0, 1.5, 2.0, 3.0, 4.0, 6.0, -0.0, -0.5, -1.0, -1.5, -2.0, -3.0, -4.0, -6.0])


def pack_weight(w, fmt):
    k, n = w.shape
    w = f64(np.asarray(w, np.float32).astype(ml_dtypes.bfloat16)).reshape(k // 32, 32, n)
    amax = np.abs(w).max(1)
    if fmt in ("e4m3", "e5m2"):
        byte = np.frexp(amax)[1] - 1 + 127 - (7 if fmt == "e4m3" else 14)
    else:
        mant, ex = np.frexp(amax / 6.0)
        byte = np.where(mant > 0.5, ex, ex - 1) + 127
    byte = np.clip(np.where(amax > 0, byte, 1), 1, 254)
    scaled = (w * np.exp2(127.0 - byte)[:, None, :]).reshape(k, n).astype(np.float32)
    by_word = np.ascontiguousarray(scaled.reshape(k // 512, 128, 4, n).transpose(0, 1, 3, 2))
    if fmt in ("e4m3", "e5m2"):
        words = by_word.astype(ml_dtypes.float8_e4m3fn if fmt == "e4m3" else ml_dtypes.float8_e5m2).view(np.uint8)
    else:
        c = by_word.astype(ml_dtypes.float4_e2m1fn).view(np.uint8) & 0xF
        words = (c[..., 0::2] | (c[..., 1::2] << 4)).reshape(k // 512, 128, 2 * n)
    return np.ascontiguousarray(words), np.ascontiguousarray(byte.astype(np.uint8).reshape(k // 512, 16, n))


def unpack_weight(words, scales, fmt):
    g, _, n = scales.shape
    words = np.ascontiguousarray(words).reshape(g, 128, n, -1)
    if fmt in ("e4m3", "e5m2"):
        vals = words.view(ml_dtypes.float8_e4m3fn if fmt == "e4m3" else ml_dtypes.float8_e5m2).astype(np.float64)
    else:
        nib = np.empty((g, 128, n, 4), np.uint8)
        nib[..., 0::2] = words & 0xF
        nib[..., 1::2] = words >> 4
        vals = E2M1[nib]
    vals = vals * np.repeat(np.exp2(scales.astype(np.float64) - 127.0), 8, axis=1)[..., None]
    return vals.transpose(0, 1, 3, 2).reshape(g * 512, n)


def sigmoid(v):
    return 1.0 / (1.0 + np.exp(-v))


def sgn(shape):
    return np.random.uniform(0.5, 2.0, shape) * np.where(np.random.standard_normal(shape) < 0, -1.0, 1.0)


K, T, J, R, I, O, N, S, E = 512, 1024, 256, 512, 256, 128, 256, 1024, 512


def setup_inputs():
    n = np.random.standard_normal
    idx = np.random.permutation(T)[:J]
    idx2 = np.random.permutation(J)[:I]
    idx3 = np.random.permutation(J)[:I]
    idx4 = np.random.permutation(S)[:N]
    idx5 = np.random.permutation(E)[:O]
    idx6 = np.random.permutation(E)[:O]
    fk = mx_kscale(K)
    fr = mx_kscale(R)
    xtp = pack_weight(n((K, T)) / fk[:, None], "e5m2")
    wp = pack_weight(n((K, R)) * 1 / np.sqrt(K) * fk[:, None], "e2m1")
    vsp = pack_weight(n((R, S)) * 1 / np.sqrt(R) / fr[:, None], "e2m1")
    return {
        "xt_words": xtp[0],
        "xt_scales": xtp[1],
        "w_words": wp[0],
        "w_scales": wp[1],
        "sa": (sgn((R, 1)) * fr[:, None]).astype(np.float32),
        "sg": (sgn((R, 1))).astype(np.float32),
        "bg": (np.random.uniform(-2.0, 2.0, (R, 1))).astype(np.float32),
        "vs_words": vsp[0],
        "vs_scales": vsp[1],
        "offs": striped(idx),
        "offs2": striped(idx2),
        "offs3": striped(idx3),
        "offs4": striped(idx4),
        "offs5": striped(idx5),
        "offs6": striped(idx6),
    }


def reference(xt_words, xt_scales, w_words, w_scales, sa, sg, bg, vs_words, vs_scales, offs, offs2, offs3, offs4, offs5, offs6):
    idx = unstriped(offs)
    idx2 = unstriped(offs2)
    idx3 = unstriped(offs3)
    idx4 = unstriped(offs4)
    idx5 = unstriped(offs5)
    idx6 = unstriped(offs6)
    xtu = unpack_weight(xt_words, xt_scales, "e5m2")
    wu = unpack_weight(w_words, w_scales, "e2m1")
    vsu = unpack_weight(vs_words, vs_scales, "e2m1")
    xtidxg = xtu[:, idx]
    a = wu.T @ xtidxg
    h1 = a[:, idx2] * f64(sa) * sigmoid(a[:, idx3] * f64(sg) + f64(bg))
    hid = h1.reshape(R, O, I // O).max(axis=2)
    vsidx4g = vsu[:, idx4]
    hidq = mxq(hid, 0, "e4m3")
    p = vsidx4g.T @ hidq
    pa = np.zeros((N, E))
    pa[:, idx5] = p
    pb = np.zeros((N, E))
    pb[:, idx6] = p
    y = pa + pb
    return y

@@ -1,0 +1,198 @@
+from contextlib import ExitStack
+
+import concourse.mybir as mybir
+
+K, T, J, R, I, O, N, S, E = 512, 1024, 256, 512, 256, 128, 256, 1024, 512
+FLOPS = 2 * K * R * J + 2 * R * N * O
+
+F32 = mybir.dt.float32
+BF16 = mybir.dt.bfloat16
+I32 = mybir.dt.int32
+U32 = mybir.dt.uint32
+U16 = mybir.dt.uint16
+U8 = mybir.dt.uint8
+E4M3 = mybir.dt.float8_e4m3fn_x4
+E5M2 = mybir.dt.float8_e5m2_x4
+E2M1 = mybir.dt.float4_e2m1fn_x4
+ACT = mybir.ActivationFunctionType
+ALU = mybir.AluOpType
+
+P = 128
+PACK = 4
+
+
+def tile_list_gatedpool_solo_store_pagetwice_kernel(
+    tc, xt_words, xt_scales, w_words, w_scales, sa, sg, bg, vs_words, vs_scales, offs, offs2, offs3, offs4, offs5, offs6, out
+):
+    nc = tc.nc
+    with ExitStack() as ctx:
+        sb = ctx.enter_context(tc.tile_pool(name="sb", bufs=1))
+        reuse = ctx.enter_context(tc.tile_pool(name="reuse", bufs=1))
+        reuse2 = ctx.enter_context(tc.tile_pool(name="reuse2", bufs=1))
+        reuse3 = ctx.enter_context(tc.tile_pool(name="reuse3", bufs=1))
+        ps = ctx.enter_context(tc.psum_pool(name="ps", bufs=1))
+
+        def load_list(src, name):
+            lst = sb.tile(list(src.shape), U16, name=name)
+            nc.sync.dma_start(lst[:], src)
+            return lst
+
+        def load_rows(src, name):
+            col = sb.tile([P, PACK], F32, name=name)
+            nc.sync.dma_start(out=col[:], in_=src.rearrange("(p t) o -> p (t o)", t=PACK))
+            return col
+
+        def load_scales(queue, plane, src):
+            for q in range(4):
+                queue.dma_start(out=plane[32 * q : 32 * q + 4, :].bitcast(I32), in_=src[0, 4 * q : 4 * q + 4, :].bitcast(I32))
+
+        xs = reuse3.tile([P, T], U8, name="xs", offset=4 * R, align_bytes=64)
+        ws = sb.tile([P, R], U8, name="ws")
+        ws_in = reuse3.tile([4, 4 * R], U8, name="ws_in", offset=0, align_bytes=64)
+        vs = reuse.tile([P, S], U8, name="vs", offset=0)
+        nc.vector.memset(xs[:].bitcast(I32), 0)
+        nc.vector.memset(ws[:].bitcast(I32), 0)
+        nc.vector.memset(vs[:].bitcast(I32), 0)
+        pages = [[sb.tile([P, E], F32, name="page0%d" % c) for c in range(2)]]
+        for c in range(2):
+            nc.vector.memset(pages[0][c][:], 0.0)
+
+        l1 = load_list(offs, "l1")
+        xw = reuse2.tile([P, T], I32, name="xw", offset=0)
+        nc.scalar.dma_start(out=xw[:], in_=xt_words[0].rearrange("p c r -> p (c r)").bitcast(I32))
+        nc.sync.dma_start(
+            out=ws_in[:].bitcast(I32).rearrange("p (q c) -> p q c", q=4),
+            in_=w_scales[0].bitcast(I32).rearrange("(q r) c -> r q c", q=4),
+        )
+        ww = sb.tile([P, R], U16, name="ww")
+        nc.sync.dma_start(out=ww[:].bitcast(I32), in_=w_words[0].bitcast(I32))
+        load_scales(nc.sync, xs, xt_scales)
+        l2 = load_list(offs2, "l2")
+        sa_t = load_rows(sa, "sa_t")
+        vw = reuse.tile([P, S], U16, name="vw", offset=S)
+        nc.sync.dma_start(out=vw[:].bitcast(I32), in_=vs_words[0].bitcast(I32))
+        l4 = load_list(offs4, "l4")
+        load_scales(nc.sync, vs, vs_scales)
+        l3 = load_list(offs3, "l3")
+        sg_t = load_rows(sg, "sg_t")
+        bg_t = load_rows(bg, "bg_t")
+        l5 = load_list(offs5, "l5")
+        l6 = load_list(offs6, "l6")
+
+
+        for q in range(4):
+            nc.vector.tensor_copy(out=ws[32 * q : 32 * q + 4, 0:R].bitcast(I32), in_=ws_in[:, q * R : (q + 1) * R].bitcast(I32))
+        xsg = reuse3.tile([P, J], U8, name="xsg", offset=0, align_bytes=64)
+        nc.vector.tensor_copy(xsg[:], xs[:].indirect(l1[:]))
+        wsp = sb.tile([P, R], U8, name="wsp", align_bytes=64)
+        wwp = sb.tile([P, R], U16, name="wwp", align_bytes=64)
+        ws_dealt = ws[:, 0:R].rearrange("p (m t) -> p t m", t=PACK)
+        ww_dealt = ww[:].rearrange("p (m t) -> p t m", t=PACK)
+        nc.vector.tensor_copy(out=wsp[:, 0:P], in_=ws_dealt[:, 0, :])
+        nc.scalar.copy(out=wwp[:, 0:P], in_=ww_dealt[:, 0, :])
+        xg = reuse3.tile([P, J], U32, name="xg", offset=4 * R, align_bytes=64)
+        for h in range(2):
+            nc.vector.tensor_copy(xg[:, P * h : P * (h + 1)], xw[:].bitcast(U32).indirect(l1[:, 8 * h : 8 * (h + 1)]))
+        nc.vector.tensor_copy(out=wsp[:, P:R].rearrange("p (t m) -> p t m", m=P), in_=ws_dealt[:, 1:PACK, :])
+        nc.scalar.copy(out=wwp[:, P:R].rearrange("p (t m) -> p t m", m=P), in_=ww_dealt[:, 1:PACK, :])
+
+        pages.append([reuse2.tile([P, E], F32, name="page1%d" % c, offset=4 * E * c) for c in range(2)])
+        for c in range(2):
+            nc.gpsimd.memset(pages[1][c][:], 0.0)
+
+        a = []
+        for t in range(PACK):
+            a_t = sb.tile([P, 2 * J], F32, name="a%d" % t)
+            parts = [(0, P), (P, J)] if t == 0 else [(0, J)]
+            for lo, hi in parts:
+                acc = ps.tile([P, hi - lo], F32, name="acc%d_%d" % (t, lo))
+                nc.tensor.matmul_mx(
+                    out=acc[:],
+                    lhsT=wwp[:, P * t : P * (t + 1)].bitcast(E2M1),
+                    lhsT_scale=wsp[:, P * t : P * (t + 1)],
+                    rhs=xg[:, lo:hi].bitcast(E5M2),
+                    rhs_scale=xsg[:, lo:hi],
+                    start=True,
+                    stop=True,
+                )
+                if t == 0:
+                    nc.scalar.copy(out=a_t[:, lo:hi], in_=acc[:])
+                else:
+                    nc.vector.tensor_copy(out=a_t[:, lo:hi], in_=acc[:])
+            a.append(a_t)
+
+        vg = sb.tile([P, N], U16, name="vg", align_bytes=64)
+        vsg = sb.tile([P, N], U8, name="vsg", align_bytes=64)
+
+        def fetch_val(t, val, lo, hi):
+            nc.scalar.activation(out=val[:, lo:hi], in_=a[t][:].indirect(l2[:, lo // 16 : hi // 16]), func=ACT.Copy, scale=sa_t[:, t : t + 1])
+
+        def fetch_gate(t, gate, lo, hi):
+            nc.scalar.activation(
+                out=gate[:, lo:hi],
+                in_=a[t][:].indirect(l3[:, lo // 16 : hi // 16]),
+                func=ACT.Sigmoid,
+                bias=bg_t[:, t : t + 1],
+                scale=sg_t[:, t : t + 1],
+            )
+
+        def pool_pair(h1, hid3, t, lo, hi):
+            pair = h1[:, :, lo:hi].rearrange("p t (o u) -> p o t u", u=2)
+            nc.vector.tensor_tensor(out=hid3[:, lo // 2 : hi // 2, t - 1 : t + 1], in0=pair[:, :, :, 0], in1=pair[:, :, :, 1], op=ALU.max)
+
+        nc.vector.tensor_copy(vg[:], vw[:].indirect(l4[:]))
+        nc.vector.tensor_copy(vsg[:], vs[:].indirect(l4[:]))
+        vals = [sb.tile([P, I], F32, name="val%d" % t) for t in range(PACK)]
+        for t in range(PACK):
+            fetch_val(t, vals[t], 0, I)
+        hid = sb.tile([P, O * PACK], BF16, name="hid", align_bytes=64)
+        hid3 = hid[:].rearrange("p (o t) -> p o t", t=PACK)
+        h1s = [reuse.tile([P, 2, I], F32, name="h1a", offset=0), sb.tile([P, 2, I], F32, name="h1b")]
+        for t in range(PACK):
+            gate = sb.tile([P, I], F32, name="gate%d" % t)
+            h1 = h1s[t // 2]
+            parts = [(0, I)] if t < PACK - 1 else [(0, I // 2), (I // 2, I)]
+            for lo, hi in parts:
+                fetch_gate(t, gate, lo, hi)
+                nc.vector.tensor_tensor(out=h1[:, t % 2, lo:hi], in0=vals[t][:, lo:hi], in1=gate[:, lo:hi], op=ALU.mult)
+            if t % 2 == 1:
+                for lo, hi in parts:
+                    pool_pair(h1, hid3, t, lo, hi)
+
+        hq = sb.tile([P, O], U32, name="hq", align_bytes=64)
+        hs = sb.tile([P, O], U8, name="hs", align_bytes=64)
+        nc.vector.quantize_mx(out=hq[:].bitcast(E4M3), scales=hs[:], in_=hid[:])
+
+        prod = []
+        for b in range(2):
+            acc = ps.tile([P, O], F32, name="res%d" % b)
+            nc.tensor.matmul_mx(
+                out=acc[:],
+                lhsT=vg[:, P * b : P * (b + 1)].bitcast(E2M1),
+                lhsT_scale=vsg[:, P * b : P * (b + 1)],
+                rhs=hq[:].bitcast(E4M3),
+                rhs_scale=hs[:],
+                start=True,
+                stop=True,
+            )
+            p_b = sb.tile([P, O], F32, name="p%d" % b)
+            if b == 0:
+                nc.vector.tensor_copy(out=p_b[:], in_=acc[:])
+            else:
+                nc.scalar.copy(out=p_b[:], in_=acc[:])
+            prod.append(p_b)
+
+        y = [sb.tile([P, E], F32, name="y%d" % b) for b in range(2)]
+        half = O // 2
+        nc.vector.tensor_copy(pages[0][0][:].indirect(l5[:]), prod[0][:])
+        nc.scalar.activation(out=pages[0][1][:].indirect(l6[:]), in_=prod[0][:], func=ACT.Copy)
+        nc.scalar.activation(out=pages[1][0][:].indirect(l5[:, 0 : half // 16]), in_=prod[1][:, 0:half], func=ACT.Copy)
+        nc.scalar.activation(out=pages[1][1][:].indirect(l6[:]), in_=prod[1][:], func=ACT.Copy)
+        nc.vector.tensor_tensor(out=y[0][:], in0=pages[0][0][:], in1=pages[0][1][:], op=ALU.add)
+        nc.sync.dma_start(out=out[0:P, :], in_=y[0][:])
+        nc.vector.tensor_copy(pages[1][0][:].indirect(l5[:, half // 16 : O // 16]), prod[1][:, half:O])
+        for h in range(2):
+            cols = slice(h * E // 2, (h + 1) * E // 2)
+            nc.vector.tensor_tensor(out=y[1][:, cols], in0=pages[1][0][:, cols], in1=pages[1][1][:, cols], op=ALU.add)
+            queue = nc.sync if h == 0 else nc.scalar
+            queue.dma_start(out=out[P : 2 * P, cols], in_=y[1][:, cols])

@@ -53,6 +53,8 @@ def tile_list_gatedpool_solo_store_pagetwice_kernel(
         nc.vector.memset(xs[:].bitcast(I32), 0)
         nc.vector.memset(ws[:].bitcast(I32), 0)
         nc.vector.memset(vs[:].bitcast(I32), 0)
+        warm = sb.tile([P, 2], F32, name="warm")
+        nc.vector.memset(warm[:, 0:1], 0.0)
         pages = [[sb.tile([P, E], F32, name="page0%d" % c) for c in range(2)]]
         for c in range(2):
             nc.vector.memset(pages[0][c][:], 0.0)
@@ -80,6 +82,7 @@ def tile_list_gatedpool_solo_store_pagetwice_kernel(
         l6 = load_list(offs6, "l6")
 
 
+        nc.scalar.activation(out=warm[:, 1:2], in_=warm[:, 0:1], func=ACT.Sigmoid)
         for q in range(4):
             nc.vector.tensor_copy(out=ws[32 * q : 32 * q + 4, 0:R].bitcast(I32), in_=ws_in[:, q * R : (q + 1) * R].bitcast(I32))
         xsg = reuse3.tile([P, J], U8, name="xsg", offset=0, align_bytes=64)

@@ -28,8 +28,8 @@ def tile_list_gatedpool_solo_store_pagetwice_kernel(
     with ExitStack() as ctx:
         sb = ctx.enter_context(tc.tile_pool(name="sb", bufs=1))
         reuse = ctx.enter_context(tc.tile_pool(name="reuse", bufs=1))
-        reuse2 = ctx.enter_context(tc.tile_pool(name="reuse2", bufs=1))
         reuse3 = ctx.enter_context(tc.tile_pool(name="reuse3", bufs=1))
+        reuse2 = ctx.enter_context(tc.tile_pool(name="reuse2", bufs=1))
         ps = ctx.enter_context(tc.psum_pool(name="ps", bufs=1))
 
         def load_list(src, name):
@@ -46,12 +46,11 @@ def tile_list_gatedpool_solo_store_pagetwice_kernel(
             for q in range(4):
                 queue.dma_start(out=plane[32 * q : 32 * q + 4, :].bitcast(I32), in_=src[0, 4 * q : 4 * q + 4, :].bitcast(I32))
 
-        xs = reuse3.tile([P, T], U8, name="xs", offset=4 * R, align_bytes=64)
-        ws = sb.tile([P, R], U8, name="ws")
-        ws_in = reuse3.tile([4, 4 * R], U8, name="ws_in", offset=0, align_bytes=64)
+        xs = reuse3.tile([P, T], U8, name="xs", offset=0, align_bytes=64)
+        ws = sb.tile([P, 2 * R], U8, name="ws")
         vs = reuse.tile([P, S], U8, name="vs", offset=0)
+        nc.vector.memset(ws[0:64, :].bitcast(I32), 0)
         nc.vector.memset(xs[:].bitcast(I32), 0)
-        nc.vector.memset(ws[:].bitcast(I32), 0)
         nc.vector.memset(vs[:].bitcast(I32), 0)
         warm = sb.tile([P, 2], F32, name="warm")
         nc.vector.memset(warm[:, 0:1], 0.0)
@@ -60,14 +59,15 @@ def tile_list_gatedpool_solo_store_pagetwice_kernel(
             nc.vector.memset(pages[0][c][:], 0.0)
 
         l1 = load_list(offs, "l1")
-        xw = reuse2.tile([P, T], I32, name="xw", offset=0)
+        xw = sb.tile([P, T], I32, name="xw")
         nc.scalar.dma_start(out=xw[:], in_=xt_words[0].rearrange("p c r -> p (c r)").bitcast(I32))
-        nc.sync.dma_start(
-            out=ws_in[:].bitcast(I32).rearrange("p (q c) -> p q c", q=4),
-            in_=w_scales[0].bitcast(I32).rearrange("(q r) c -> r q c", q=4),
-        )
+        for q in range(2):
+            nc.sync.dma_start(
+                out=ws[32 * q : 32 * q + 4, :].bitcast(I32).rearrange("p (g c) -> p g c", g=2),
+                in_=w_scales[0].bitcast(I32).rearrange("(g q r) c -> q r g c", g=2, q=2)[q],
+            )
         ww = sb.tile([P, R], U16, name="ww")
-        nc.sync.dma_start(out=ww[:].bitcast(I32), in_=w_words[0].bitcast(I32))
+        nc.gpsimd.dma_start(out=ww[:].bitcast(I32), in_=w_words[0].bitcast(I32))
         load_scales(nc.sync, xs, xt_scales)
         l2 = load_list(offs2, "l2")
         sa_t = load_rows(sa, "sa_t")
@@ -83,25 +83,20 @@ def tile_list_gatedpool_solo_store_pagetwice_kernel(
 
 
         nc.scalar.activation(out=warm[:, 1:2], in_=warm[:, 0:1], func=ACT.Sigmoid)
-        for q in range(4):
-            nc.vector.tensor_copy(out=ws[32 * q : 32 * q + 4, 0:R].bitcast(I32), in_=ws_in[:, q * R : (q + 1) * R].bitcast(I32))
-        xsg = reuse3.tile([P, J], U8, name="xsg", offset=0, align_bytes=64)
+        nc.vector.tensor_copy(out=ws[64:128, 0:R].bitcast(I32), in_=ws[0:64, R : 2 * R].bitcast(I32))
+        xsg = sb.tile([P, J], U8, name="xsg", tag="picked_scales", align_bytes=64)
         nc.vector.tensor_copy(xsg[:], xs[:].indirect(l1[:]))
-        wsp = sb.tile([P, R], U8, name="wsp", align_bytes=64)
-        wwp = sb.tile([P, R], U16, name="wwp", align_bytes=64)
+        wsp = reuse2.tile([P, R], U8, name="wsp", offset=4 * E, align_bytes=64)
+        wwp = reuse2.tile([P, R], U16, name="wwp", offset=0, align_bytes=64)
         ws_dealt = ws[:, 0:R].rearrange("p (m t) -> p t m", t=PACK)
         ww_dealt = ww[:].rearrange("p (m t) -> p t m", t=PACK)
         nc.vector.tensor_copy(out=wsp[:, 0:P], in_=ws_dealt[:, 0, :])
         nc.scalar.copy(out=wwp[:, 0:P], in_=ww_dealt[:, 0, :])
-        xg = reuse3.tile([P, J], U32, name="xg", offset=4 * R, align_bytes=64)
+        xg = reuse3.tile([P, J], U32, name="xg", offset=0, align_bytes=64)
         for h in range(2):
             nc.vector.tensor_copy(xg[:, P * h : P * (h + 1)], xw[:].bitcast(U32).indirect(l1[:, 8 * h : 8 * (h + 1)]))
         nc.vector.tensor_copy(out=wsp[:, P:R].rearrange("p (t m) -> p t m", m=P), in_=ws_dealt[:, 1:PACK, :])
         nc.scalar.copy(out=wwp[:, P:R].rearrange("p (t m) -> p t m", m=P), in_=ww_dealt[:, 1:PACK, :])
-
-        pages.append([reuse2.tile([P, E], F32, name="page1%d" % c, offset=4 * E * c) for c in range(2)])
-        for c in range(2):
-            nc.gpsimd.memset(pages[1][c][:], 0.0)
 
         a = []
         for t in range(PACK):
@@ -124,8 +119,11 @@ def tile_list_gatedpool_solo_store_pagetwice_kernel(
                     nc.vector.tensor_copy(out=a_t[:, lo:hi], in_=acc[:])
             a.append(a_t)
 
-        vg = sb.tile([P, N], U16, name="vg", align_bytes=64)
-        vsg = sb.tile([P, N], U8, name="vsg", align_bytes=64)
+        pages.append([reuse2.tile([P, E], F32, name="page1%d" % c, offset=4 * E * c, align_bytes=64) for c in range(2)])
+        for c in range(2):
+            nc.gpsimd.memset(pages[1][c][:], 0.0)
+        vg = reuse3.tile([P, N], U16, name="vg", offset=0, align_bytes=64)
+        vsg = sb.tile([P, N], U8, name="vsg", tag="picked_scales", align_bytes=64)
 
         def fetch_val(t, val, lo, hi):
             nc.scalar.activation(out=val[:, lo:hi], in_=a[t][:].indirect(l2[:, lo // 16 : hi // 16]), func=ACT.Copy, scale=sa_t[:, t : t + 1])

@@ -59,7 +59,7 @@ def tile_list_gatedpool_solo_store_pagetwice_kernel(
             nc.vector.memset(pages[0][c][:], 0.0)
 
         l1 = load_list(offs, "l1")
-        xw = sb.tile([P, T], I32, name="xw")
+        xw = sb.tile([P, T], I32, name="xw", tag="xw", align_bytes=64)
         nc.scalar.dma_start(out=xw[:], in_=xt_words[0].rearrange("p c r -> p (c r)").bitcast(I32))
         for q in range(2):
             nc.sync.dma_start(
@@ -86,16 +86,17 @@ def tile_list_gatedpool_solo_store_pagetwice_kernel(
         nc.vector.tensor_copy(out=ws[64:128, 0:R].bitcast(I32), in_=ws[0:64, R : 2 * R].bitcast(I32))
         xsg = sb.tile([P, J], U8, name="xsg", tag="picked_scales", align_bytes=64)
         nc.vector.tensor_copy(xsg[:], xs[:].indirect(l1[:]))
-        wsp = reuse2.tile([P, R], U8, name="wsp", offset=4 * E, align_bytes=64)
-        wwp = reuse2.tile([P, R], U16, name="wwp", offset=0, align_bytes=64)
+        wsp0 = reuse2.tile([P, 2 * P], U8, name="wsp0", offset=8 * E, align_bytes=64)
+        wwp = reuse2.tile([P, R], U16, name="wwp", offset=4 * E - R, align_bytes=64)
         ws_dealt = ws[:, 0:R].rearrange("p (m t) -> p t m", t=PACK)
         ww_dealt = ww[:].rearrange("p (m t) -> p t m", t=PACK)
-        nc.vector.tensor_copy(out=wsp[:, 0:P], in_=ws_dealt[:, 0, :])
+        nc.vector.tensor_copy(out=wsp0[:].rearrange("p (t m) -> p t m", m=P), in_=ws_dealt[:, 0:2, :])
         nc.scalar.copy(out=wwp[:, 0:P], in_=ww_dealt[:, 0, :])
         xg = reuse3.tile([P, J], U32, name="xg", offset=0, align_bytes=64)
         for h in range(2):
             nc.vector.tensor_copy(xg[:, P * h : P * (h + 1)], xw[:].bitcast(U32).indirect(l1[:, 8 * h : 8 * (h + 1)]))
-        nc.vector.tensor_copy(out=wsp[:, P:R].rearrange("p (t m) -> p t m", m=P), in_=ws_dealt[:, 1:PACK, :])
+        wsp = sb.tile([P, 2 * P], U8, name="wsp", tag="xw", align_bytes=64)
+        nc.vector.tensor_copy(out=wsp[:].rearrange("p (t m) -> p t m", m=P), in_=ws_dealt[:, 2:PACK, :])
         nc.scalar.copy(out=wwp[:, P:R].rearrange("p (t m) -> p t m", m=P), in_=ww_dealt[:, 1:PACK, :])
 
         a = []
@@ -107,7 +108,7 @@ def tile_list_gatedpool_solo_store_pagetwice_kernel(
                 nc.tensor.matmul_mx(
                     out=acc[:],
                     lhsT=wwp[:, P * t : P * (t + 1)].bitcast(E2M1),
-                    lhsT_scale=wsp[:, P * t : P * (t + 1)],
+                    lhsT_scale=[wsp0, wsp][t // 2][:, P * (t % 2) : P * (t % 2 + 1)],
                     rhs=xg[:, lo:hi].bitcast(E5M2),
                     rhs_scale=xsg[:, lo:hi],
                     start=True,
@@ -149,49 +150,54 @@ def tile_list_gatedpool_solo_store_pagetwice_kernel(
         hid = sb.tile([P, O * PACK], BF16, name="hid", align_bytes=64)
         hid3 = hid[:].rearrange("p (o t) -> p o t", t=PACK)
         h1s = [reuse.tile([P, 2, I], F32, name="h1a", offset=0), sb.tile([P, 2, I], F32, name="h1b")]
-        for t in range(PACK):
-            gate = sb.tile([P, I], F32, name="gate%d" % t)
-            h1 = h1s[t // 2]
-            parts = [(0, I)] if t < PACK - 1 else [(0, I // 2), (I // 2, I)]
-            for lo, hi in parts:
-                fetch_gate(t, gate, lo, hi)
-                nc.vector.tensor_tensor(out=h1[:, t % 2, lo:hi], in0=vals[t][:, lo:hi], in1=gate[:, lo:hi], op=ALU.mult)
-            if t % 2 == 1:
-                for lo, hi in parts:
-                    pool_pair(h1, hid3, t, lo, hi)
+        half = O // 2
+        hq = sb.tile([P, half + O], U32, name="hq", align_bytes=64)
+        hs = sb.tile([P, half + O], U8, name="hs", align_bytes=64)
+        nc.vector.memset(hq[:, 0:half].bitcast(I32), 0)
+        nc.vector.memset(hs[:, 0:half].bitcast(I32), 0)
+        gates = [sb.tile([P, I], F32, name="gate%d" % t) for t in range(PACK)]
 
-        hq = sb.tile([P, O], U32, name="hq", align_bytes=64)
-        hs = sb.tile([P, O], U8, name="hs", align_bytes=64)
-        nc.vector.quantize_mx(out=hq[:].bitcast(E4M3), scales=hs[:], in_=hid[:])
-
-        prod = []
-        for b in range(2):
-            acc = ps.tile([P, O], F32, name="res%d" % b)
+        def product(name, b, col):
+            acc = ps.tile([P, O], F32, name=name)
             nc.tensor.matmul_mx(
                 out=acc[:],
                 lhsT=vg[:, P * b : P * (b + 1)].bitcast(E2M1),
                 lhsT_scale=vsg[:, P * b : P * (b + 1)],
-                rhs=hq[:].bitcast(E4M3),
-                rhs_scale=hs[:],
+                rhs=hq[:, col : col + O].bitcast(E4M3),
+                rhs_scale=hs[:, col : col + O],
                 start=True,
                 stop=True,
             )
-            p_b = sb.tile([P, O], F32, name="p%d" % b)
-            if b == 0:
-                nc.vector.tensor_copy(out=p_b[:], in_=acc[:])
-            else:
-                nc.scalar.copy(out=p_b[:], in_=acc[:])
-            prod.append(p_b)
+            return acc
 
+        prod = [sb.tile([P, O], F32, name="p%d" % b) for b in range(2)]
+        lists = [l5, l6]
+        for h in range(2):
+            lo, hi = h * I // 2, (h + 1) * I // 2
+            for t in range(PACK):
+                h1 = h1s[t // 2]
+                fetch_gate(t, gates[t], lo, hi)
+                nc.vector.tensor_tensor(out=h1[:, t % 2, lo:hi], in0=vals[t][:, lo:hi], in1=gates[t][:, lo:hi], op=ALU.mult)
+                if t % 2 == 1:
+                    pool_pair(h1, hid3, t, lo, hi)
+            cols = slice(half * (h + 1), half * (h + 2))
+            nc.vector.quantize_mx(out=hq[:, cols].bitcast(E4M3), scales=hs[:, cols], in_=hid[:, PACK * half * h : PACK * half * (h + 1)])
+            if h == 0:
+                early = product("early", 0, 0)
+        nc.scalar.copy(out=prod[0][:, 0:half], in_=early[:, half:O])
+        for c in range(2):
+            nc.scalar.activation(out=pages[0][c][:].indirect(lists[c][:, 0 : half // 16]), in_=prod[0][:, 0:half], func=ACT.Copy)
+        late = [product("res%d" % b, b, half) for b in (1, 0)]
+        nc.scalar.copy(out=prod[1][:], in_=late[0][:])
+        nc.vector.tensor_copy(out=prod[0][:, half:O], in_=late[1][:, half:O])
         y = [sb.tile([P, E], F32, name="y%d" % b) for b in range(2)]
-        half = O // 2
-        nc.vector.tensor_copy(pages[0][0][:].indirect(l5[:]), prod[0][:])
-        nc.scalar.activation(out=pages[0][1][:].indirect(l6[:]), in_=prod[0][:], func=ACT.Copy)
         nc.scalar.activation(out=pages[1][0][:].indirect(l5[:, 0 : half // 16]), in_=prod[1][:, 0:half], func=ACT.Copy)
         nc.scalar.activation(out=pages[1][1][:].indirect(l6[:]), in_=prod[1][:], func=ACT.Copy)
+        for c in range(2):
+            nc.vector.tensor_copy(pages[0][c][:].indirect(lists[c][:, half // 16 : O // 16]), prod[0][:, half:O])
+        nc.vector.tensor_copy(pages[1][0][:].indirect(l5[:, half // 16 : O // 16]), prod[1][:, half:O])
         nc.vector.tensor_tensor(out=y[0][:], in0=pages[0][0][:], in1=pages[0][1][:], op=ALU.add)
         nc.sync.dma_start(out=out[0:P, :], in_=y[0][:])
-        nc.vector.tensor_copy(pages[1][0][:].indirect(l5[:, half // 16 : O // 16]), prod[1][:, half:O])
         for h in range(2):
             cols = slice(h * E // 2, (h + 1) * E // 2)
             nc.vector.tensor_tensor(out=y[1][:, cols], in0=pages[1][0][:, cols], in1=pages[1][1][:, cols], op=ALU.add)

@@ -191,11 +191,9 @@ def tile_list_gatedpool_solo_store_pagetwice_kernel(
         nc.scalar.copy(out=prod[1][:], in_=late[0][:])
         nc.vector.tensor_copy(out=prod[0][:, half:O], in_=late[1][:, half:O])
         y = [sb.tile([P, E], F32, name="y%d" % b) for b in range(2)]
-        nc.scalar.activation(out=pages[1][0][:].indirect(l5[:, 0 : half // 16]), in_=prod[1][:, 0:half], func=ACT.Copy)
-        nc.scalar.activation(out=pages[1][1][:].indirect(l6[:]), in_=prod[1][:], func=ACT.Copy)
         for c in range(2):
+            nc.scalar.activation(out=pages[1][c][:].indirect(lists[c][:]), in_=prod[1][:], func=ACT.Copy)
             nc.vector.tensor_copy(pages[0][c][:].indirect(lists[c][:, half // 16 : O // 16]), prod[0][:, half:O])
-        nc.vector.tensor_copy(pages[1][0][:].indirect(l5[:, half // 16 : O // 16]), prod[1][:, half:O])
         nc.vector.tensor_tensor(out=y[0][:], in0=pages[0][0][:], in1=pages[0][1][:], op=ALU.add)
         nc.sync.dma_start(out=out[0:P, :], in_=y[0][:])
         for h in range(2):

from contextlib import ExitStack

import concourse.mybir as mybir

K, T, J, R, I, O, N, S, E = 512, 1024, 256, 512, 256, 128, 256, 1024, 512
FLOPS = 2 * K * R * J + 2 * R * N * O

F32 = mybir.dt.float32
BF16 = mybir.dt.bfloat16
I32 = mybir.dt.int32
U32 = mybir.dt.uint32
U16 = mybir.dt.uint16
U8 = mybir.dt.uint8
E4M3 = mybir.dt.float8_e4m3fn_x4
E5M2 = mybir.dt.float8_e5m2_x4
E2M1 = mybir.dt.float4_e2m1fn_x4
ACT = mybir.ActivationFunctionType
ALU = mybir.AluOpType

P = 128
PACK = 4


def tile_list_gatedpool_solo_store_pagetwice_kernel(
    tc, xt_words, xt_scales, w_words, w_scales, sa, sg, bg, vs_words, vs_scales, offs, offs2, offs3, offs4, offs5, offs6, out
):
    nc = tc.nc
    with ExitStack() as ctx:
        sb = ctx.enter_context(tc.tile_pool(name="sb", bufs=1))
        reuse = ctx.enter_context(tc.tile_pool(name="reuse", bufs=1))
        reuse3 = ctx.enter_context(tc.tile_pool(name="reuse3", bufs=1))
        reuse2 = ctx.enter_context(tc.tile_pool(name="reuse2", bufs=1))
        ps = ctx.enter_context(tc.psum_pool(name="ps", bufs=1))

        def load_list(src, name):
            lst = sb.tile(list(src.shape), U16, name=name)
            nc.sync.dma_start(lst[:], src)
            return lst

        def load_rows(src, name):
            col = sb.tile([P, PACK], F32, name=name)
            nc.sync.dma_start(out=col[:], in_=src.rearrange("(p t) o -> p (t o)", t=PACK))
            return col

        def load_scales(queue, plane, src):
            for q in range(4):
                queue.dma_start(out=plane[32 * q : 32 * q + 4, :].bitcast(I32), in_=src[0, 4 * q : 4 * q + 4, :].bitcast(I32))

        xs = reuse3.tile([P, T], U8, name="xs", offset=0, align_bytes=64)
        ws = sb.tile([P, 2 * R], U8, name="ws")
        vs = reuse.tile([P, S], U8, name="vs", offset=0)
        nc.vector.memset(ws[0:64, :].bitcast(I32), 0)
        nc.vector.memset(xs[:].bitcast(I32), 0)
        nc.vector.memset(vs[:].bitcast(I32), 0)
        warm = sb.tile([P, 2], F32, name="warm")
        nc.vector.memset(warm[:, 0:1], 0.0)
        pages = [[sb.tile([P, E], F32, name="page0%d" % c) for c in range(2)]]
        for c in range(2):
            nc.vector.memset(pages[0][c][:], 0.0)

        l1 = load_list(offs, "l1")
        xw = sb.tile([P, T], I32, name="xw", tag="xw", align_bytes=64)
        nc.scalar.dma_start(out=xw[:], in_=xt_words[0].rearrange("p c r -> p (c r)").bitcast(I32))
        for q in range(2):
            nc.sync.dma_start(
                out=ws[32 * q : 32 * q + 4, :].bitcast(I32).rearrange("p (g c) -> p g c", g=2),
                in_=w_scales[0].bitcast(I32).rearrange("(g q r) c -> q r g c", g=2, q=2)[q],
            )
        ww = sb.tile([P, R], U16, name="ww")
        nc.gpsimd.dma_start(out=ww[:].bitcast(I32), in_=w_words[0].bitcast(I32))
        load_scales(nc.sync, xs, xt_scales)
        l2 = load_list(offs2, "l2")
        sa_t = load_rows(sa, "sa_t")
        vw = reuse.tile([P, S], U16, name="vw", offset=S)
        nc.sync.dma_start(out=vw[:].bitcast(I32), in_=vs_words[0].bitcast(I32))
        l4 = load_list(offs4, "l4")
        load_scales(nc.sync, vs, vs_scales)
        l3 = load_list(offs3, "l3")
        sg_t = load_rows(sg, "sg_t")
        bg_t = load_rows(bg, "bg_t")
        l5 = load_list(offs5, "l5")
        l6 = load_list(offs6, "l6")


        nc.scalar.activation(out=warm[:, 1:2], in_=warm[:, 0:1], func=ACT.Sigmoid)
        nc.vector.tensor_copy(out=ws[64:128, 0:R].bitcast(I32), in_=ws[0:64, R : 2 * R].bitcast(I32))
        xsg = sb.tile([P, J], U8, name="xsg", tag="picked_scales", align_bytes=64)
        nc.vector.tensor_copy(xsg[:], xs[:].indirect(l1[:]))
        wsp0 = reuse2.tile([P, 2 * P], U8, name="wsp0", offset=8 * E, align_bytes=64)
        wwp = reuse2.tile([P, R], U16, name="wwp", offset=4 * E - R, align_bytes=64)
        ws_dealt = ws[:, 0:R].rearrange("p (m t) -> p t m", t=PACK)
        ww_dealt = ww[:].rearrange("p (m t) -> p t m", t=PACK)
        nc.vector.tensor_copy(out=wsp0[:].rearrange("p (t m) -> p t m", m=P), in_=ws_dealt[:, 0:2, :])
        nc.scalar.copy(out=wwp[:, 0:P], in_=ww_dealt[:, 0, :])
        xg = reuse3.tile([P, J], U32, name="xg", offset=0, align_bytes=64)
        for h in range(2):
            nc.vector.tensor_copy(xg[:, P * h : P * (h + 1)], xw[:].bitcast(U32).indirect(l1[:, 8 * h : 8 * (h + 1)]))
        wsp = sb.tile([P, 2 * P], U8, name="wsp", tag="xw", align_bytes=64)
        nc.vector.tensor_copy(out=wsp[:].rearrange("p (t m) -> p t m", m=P), in_=ws_dealt[:, 2:PACK, :])
        nc.scalar.copy(out=wwp[:, P:R].rearrange("p (t m) -> p t m", m=P), in_=ww_dealt[:, 1:PACK, :])

        a = []
        for t in range(PACK):
            a_t = sb.tile([P, 2 * J], F32, name="a%d" % t)
            parts = [(0, P), (P, J)] if t == 0 else [(0, J)]
            for lo, hi in parts:
                acc = ps.tile([P, hi - lo], F32, name="acc%d_%d" % (t, lo))
                nc.tensor.matmul_mx(
                    out=acc[:],
                    lhsT=wwp[:, P * t : P * (t + 1)].bitcast(E2M1),
                    lhsT_scale=[wsp0, wsp][t // 2][:, P * (t % 2) : P * (t % 2 + 1)],
                    rhs=xg[:, lo:hi].bitcast(E5M2),
                    rhs_scale=xsg[:, lo:hi],
                    start=True,
                    stop=True,
                )
                if t == 0:
                    nc.scalar.copy(out=a_t[:, lo:hi], in_=acc[:])
                else:
                    nc.vector.tensor_copy(out=a_t[:, lo:hi], in_=acc[:])
            a.append(a_t)

        pages.append([reuse2.tile([P, E], F32, name="page1%d" % c, offset=4 * E * c, align_bytes=64) for c in range(2)])
        for c in range(2):
            nc.gpsimd.memset(pages[1][c][:], 0.0)
        vg = reuse3.tile([P, N], U16, name="vg", offset=0, align_bytes=64)
        vsg = sb.tile([P, N], U8, name="vsg", tag="picked_scales", align_bytes=64)

        def fetch_val(t, val, lo, hi):
            nc.scalar.activation(out=val[:, lo:hi], in_=a[t][:].indirect(l2[:, lo // 16 : hi // 16]), func=ACT.Copy, scale=sa_t[:, t : t + 1])

        def fetch_gate(t, gate, lo, hi):
            nc.scalar.activation(
                out=gate[:, lo:hi],
                in_=a[t][:].indirect(l3[:, lo // 16 : hi // 16]),
                func=ACT.Sigmoid,
                bias=bg_t[:, t : t + 1],
                scale=sg_t[:, t : t + 1],
            )

        def pool_pair(h1, hid3, t, lo, hi):
            pair = h1[:, :, lo:hi].rearrange("p t (o u) -> p o t u", u=2)
            nc.vector.tensor_tensor(out=hid3[:, lo // 2 : hi // 2, t - 1 : t + 1], in0=pair[:, :, :, 0], in1=pair[:, :, :, 1], op=ALU.max)

        nc.vector.tensor_copy(vg[:], vw[:].indirect(l4[:]))
        nc.vector.tensor_copy(vsg[:], vs[:].indirect(l4[:]))
        vals = [sb.tile([P, I], F32, name="val%d" % t) for t in range(PACK)]
        for t in range(PACK):
            fetch_val(t, vals[t], 0, I)
        hid = sb.tile([P, O * PACK], BF16, name="hid", align_bytes=64)
        hid3 = hid[:].rearrange("p (o t) -> p o t", t=PACK)
        h1s = [reuse.tile([P, 2, I], F32, name="h1a", offset=0), sb.tile([P, 2, I], F32, name="h1b")]
        half = O // 2
        hq = sb.tile([P, half + O], U32, name="hq", align_bytes=64)
        hs = sb.tile([P, half + O], U8, name="hs", align_bytes=64)
        nc.vector.memset(hq[:, 0:half].bitcast(I32), 0)
        nc.vector.memset(hs[:, 0:half].bitcast(I32), 0)
        gates = [sb.tile([P, I], F32, name="gate%d" % t) for t in range(PACK)]

        def product(name, b, col):
            acc = ps.tile([P, O], F32, name=name)
            nc.tensor.matmul_mx(
                out=acc[:],
                lhsT=vg[:, P * b : P * (b + 1)].bitcast(E2M1),
                lhsT_scale=vsg[:, P * b : P * (b + 1)],
                rhs=hq[:, col : col + O].bitcast(E4M3),
                rhs_scale=hs[:, col : col + O],
                start=True,
                stop=True,
            )
            return acc

        prod = [sb.tile([P, O], F32, name="p%d" % b) for b in range(2)]
        lists = [l5, l6]
        for h in range(2):
            lo, hi = h * I // 2, (h + 1) * I // 2
            for t in range(PACK):
                h1 = h1s[t // 2]
                fetch_gate(t, gates[t], lo, hi)
                nc.vector.tensor_tensor(out=h1[:, t % 2, lo:hi], in0=vals[t][:, lo:hi], in1=gates[t][:, lo:hi], op=ALU.mult)
                if t % 2 == 1:
                    pool_pair(h1, hid3, t, lo, hi)
            cols = slice(half * (h + 1), half * (h + 2))
            nc.vector.quantize_mx(out=hq[:, cols].bitcast(E4M3), scales=hs[:, cols], in_=hid[:, PACK * half * h : PACK * half * (h + 1)])
            if h == 0:
                early = product("early", 0, 0)
        nc.scalar.copy(out=prod[0][:, 0:half], in_=early[:, half:O])
        for c in range(2):
            nc.scalar.activation(out=pages[0][c][:].indirect(lists[c][:, 0 : half // 16]), in_=prod[0][:, 0:half], func=ACT.Copy)
        late = [product("res%d" % b, b, half) for b in (1, 0)]
        nc.scalar.copy(out=prod[1][:], in_=late[0][:])
        nc.vector.tensor_copy(out=prod[0][:, half:O], in_=late[1][:, half:O])
        y = [sb.tile([P, E], F32, name="y%d" % b) for b in range(2)]
        for c in range(2):
            nc.scalar.activation(out=pages[1][c][:].indirect(lists[c][:]), in_=prod[1][:], func=ACT.Copy)
            nc.vector.tensor_copy(pages[0][c][:].indirect(lists[c][:, half // 16 : O // 16]), prod[0][:, half:O])
        nc.vector.tensor_tensor(out=y[0][:], in0=pages[0][0][:], in1=pages[0][1][:], op=ALU.add)
        nc.sync.dma_start(out=out[0:P, :], in_=y[0][:])
        for h in range(2):
            cols = slice(h * E // 2, (h + 1) * E // 2)
            nc.vector.tensor_tensor(out=y[1][:, cols], in0=pages[1][0][:, cols], in1=pages[1][1][:, cols], op=ALU.add)
            queue = nc.sync if h == 0 else nc.scalar
            queue.dma_start(out=out[P : 2 * P, cols], in_=y[1][:, cols])
